import numpy as np
import ml_dtypes


def mxq(x, axis, fmt="e4m3"):
    dtype, down = {"e4m3": (ml_dtypes.float8_e4m3fn, 7), "e5m2": (ml_dtypes.float8_e5m2, 14)}[fmt]
    v = np.moveaxis(np.asarray(x, np.float32).astype(ml_dtypes.bfloat16).astype(np.float64), axis, -1)
    blocks = v.reshape(v.shape[:-1] + (-1, 32))
    amax = np.abs(blocks).max(-1, keepdims=True)
    byte = np.maximum(np.where(amax > 0, np.frexp(amax)[1] - 1 + 127, 0) - down, 1)
    scale = np.exp2(byte - 127.0)
    codes = (blocks / scale).astype(np.float32).astype(dtype).astype(np.float64)
    return np.moveaxis((codes * scale).reshape(v.shape), -1, axis)


WIDE = False


def mx_kscale(k):
    if not WIDE:
        return np.ones(k)
    levels = np.array([10, -10, 5, -5, 0])
    if k % 512:
        return np.exp2(np.random.permutation(np.resize(levels, k // 32))).repeat(32)
    a = np.empty((k // 512, 16))
    for p in range(k // 512):
        a[p, :8] = np.random.permutation(np.resize(levels, 8))
        for g in range(8):
            far = levels[np.abs(levels - a[p, g]) >= 10]
            a[p, g + 8] = far[np.random.randint(len(far))]
    return np.exp2(a.ravel()).repeat(32)


def f64(x):
    return np.asarray(x).astype(np.float64)


def striped(idx):
    return np.tile(np.asarray(idx).reshape(-1, 16).T, (8, 1)).astype(np.uint16)


def unstriped(offs):
    return offs[:16].T.reshape(-1).astype(np.int64)


E2M1 = np.array([0.0, 0.5, 1.0, 1.5, 2.0, 3.0, 4.0, 6.0, -0.0, -0.5, -1.0, -1.5, -2.0, -3.0, -4.0, -6.0])


def pack_weight(w, fmt):
    k, n = w.shape
    w = f64(np.asarray(w, np.float32).astype(ml_dtypes.bfloat16)).reshape(k // 32, 32, n)
    amax = np.abs(w).max(1)
    if fmt == "e4m3":
        byte = np.frexp(amax)[1] - 1 + 127 - 7
    else:
        mant, ex = np.frexp(amax / 6.0)
        byte = np.where(mant > 0.5, ex, ex - 1) + 127
    byte = np.clip(np.where(amax > 0, byte, 1), 1, 254)
    scaled = (w * np.exp2(127.0 - byte)[:, None, :]).reshape(k, n).astype(np.float32)
    by_word = np.ascontiguousarray(scaled.reshape(k // 512, 128, 4, n).transpose(0, 1, 3, 2))
    if fmt == "e4m3":
        words = by_word.astype(ml_dtypes.float8_e4m3fn).view(np.uint8)
    else:
        c = by_word.astype(ml_dtypes.float4_e2m1fn).view(np.uint8) & 0xF
        words = (c[..., 0::2] | (c[..., 1::2] << 4)).reshape(k // 512, 128, 2 * n)
    return np.ascontiguousarray(words), np.ascontiguousarray(byte.astype(np.uint8).reshape(k // 512, 16, n))


def unpack_weight(words, scales, fmt):
    g, _, n = scales.shape
    words = np.ascontiguousarray(words).reshape(g, 128, n, -1)
    if fmt == "e4m3":
        vals = words.view(ml_dtypes.float8_e4m3fn).astype(np.float64)
    else:
        nib = np.empty((g, 128, n, 4), np.uint8)
        nib[..., 0::2] = words & 0xF
        nib[..., 1::2] = words >> 4
        vals = E2M1[nib]
    vals = vals * np.repeat(np.exp2(scales.astype(np.float64) - 127.0), 8, axis=1)[..., None]
    return vals.transpose(0, 1, 3, 2).reshape(g * 512, n)


K, T, J, I, N = 1024, 1024, 512, 512, 512


def setup_inputs():
    n = np.random.standard_normal
    idx = np.random.permutation(T)[:J]
    idx2 = np.random.permutation(T)[:I]
    fk = mx_kscale(K)
    xqp = pack_weight(n((K, T)) / fk[:, None], "e4m3")
    wbp = pack_weight(n((K, N)) * 1 / np.sqrt(K) * fk[:, None], "e2m1")
    return {
        "xq_words": xqp[0],
        "xq_scales": xqp[1],
        "wa": (n((K, N)) * 1 / np.sqrt(K) * fk[:, None]).astype(np.float32),
        "wb_words": wbp[0],
        "wb_scales": wbp[1],
        "ga": (np.random.uniform(0.2, 0.9, (1, J))).astype(np.float32),
        "gb": (np.random.uniform(0.2, 0.9, (1, I))).astype(np.float32),
        "res": (1.0 * n((N, T))).astype(np.float32),
        "offs": striped(idx),
        "offs2": striped(idx2),
    }


def reference(xq_words, xq_scales, wa, wb_words, wb_scales, ga, gb, res, offs, offs2):
    idx = unstriped(offs)
    idx2 = unstriped(offs2)
    xqu = unpack_weight(xq_words, xq_scales, "e4m3")
    wbu = unpack_weight(wb_words, wb_scales, "e2m1")
    waq = mxq(f64(wa), 0, "e4m3")
    xqidxg = xqu[:, idx]
    p = waq.T @ xqidxg
    xqidx2g = xqu[:, idx2]
    q = wbu.T @ xqidx2g
    pw = p * f64(ga)
    qw = q * f64(gb)
    pg = np.zeros((N, T))
    pg[:, idx] = pw
    qg = np.zeros((N, T))
    qg[:, idx2] = qw
    y = np.maximum(pg, qg) + f64(res)
    return y

@@ -1,0 +1,262 @@
+from contextlib import ExitStack
+
+import concourse.mybir as mybir
+from concourse.masks import make_identity
+
+K, T, J, N = 1024, 1024, 512, 512
+FLOPS = 2 * 2 * K * J * N
+
+F32 = mybir.dt.float32
+BF16 = mybir.dt.bfloat16
+I32 = mybir.dt.int32
+U32 = mybir.dt.uint32
+U16 = mybir.dt.uint16
+U8 = mybir.dt.uint8
+FP8X4 = mybir.dt.float8_e4m3fn_x4
+FP4X4 = mybir.dt.float4_e2m1fn_x4
+ALU = mybir.AluOpType
+ACT = mybir.ActivationFunctionType
+
+P = 128
+PACK = 4
+PASSES = K // (P * PACK)
+TILES = N // P
+BANK = 512
+HALF_N = N // 2
+
+
+def tile_list_experts_strongest_kernel(
+    tc, xq_words, xq_scales, wa, wb_words, wb_scales, ga, gb, res, offs, offs2, out
+):
+    nc = tc.nc
+    with ExitStack() as ctx:
+        keep = ctx.enter_context(tc.tile_pool(name="keep", bufs=1))
+        ring = ctx.enter_context(tc.tile_pool(name="ring", bufs=2))
+        psum = ctx.enter_context(tc.psum_pool(name="psum", bufs=2))
+
+        list_a = keep.tile([P, J // 16], U16, name="list_a")
+        list_b = keep.tile([P, J // 16], U16, name="list_b")
+        x_words = [keep.tile([P, T], U32, name="x_words%d" % z, tag="x_words%d" % z, align_bytes=64) for z in range(PASSES)]
+        x_scales = keep.tile([P, T], U8, name="x_scales", tag="x_scales", align_bytes=64)
+        b_words = keep.tile([P, PASSES, 2 * N], U8, name="b_words", align_bytes=64)
+        b_scales = keep.tile([P, PASSES, N], U8, name="b_scales", align_bytes=64)
+        xb_scales1 = keep.tile([P, J], U8, name="xb_scales1", align_bytes=64)
+        pages_b = [keep.tile([P, T], F32, name="page_b0")]
+        ident = keep.tile([P, P], F32, name="ident")
+
+        nc.vector.memset(x_scales[:].bitcast(I32), 0)
+        nc.vector.memset(b_scales[:].rearrange("p z n -> p (z n)").bitcast(I32), 0)
+        nc.vector.memset(xb_scales1[:].bitcast(I32), 0)
+        make_identity(nc, ident[:])
+
+        def load_x_words(z):
+            nc.sync.dma_start(
+                out=x_words[z][:].bitcast(I32),
+                in_=xq_words[z].rearrange("p t r -> p (t r)").bitcast(I32),
+            )
+
+        nc.sync.dma_start(list_b[:], offs2)
+        load_x_words(0)
+        for q in range(4):
+            nc.sync.dma_start(
+                out=x_scales[32 * q : 32 * q + 8, :].bitcast(I32),
+                in_=xq_scales[:, 4 * q : 4 * q + 4, :].bitcast(I32),
+            )
+        load_x_words(1)
+        nc.sync.dma_start(list_a[:], offs)
+        for q in range(4):
+            nc.sync.dma_start(
+                out=b_scales[32 * q : 32 * q + 4, :, :].bitcast(I32),
+                in_=wb_scales[:, 4 * q : 4 * q + 4, :].rearrange("z r n -> r z n").bitcast(I32),
+            )
+        nc.sync.dma_start(
+            out=b_words[:].bitcast(I32), in_=wb_words.rearrange("z p n -> p z n").bitcast(I32)
+        )
+
+        def load_gate(g, name):
+            col = keep.tile([P, 4], F32, name=name)
+            nc.sync.dma_start(out=col[:], in_=g[0].rearrange("(p m) -> p m", m=4))
+            return col
+
+        def load_wa(h, z):
+            raw = keep.tile([P, PACK, HALF_N], F32, name="raw%d%d" % (h, z), tag="stage%d%d" % (h, z))
+            rows = wa[z * P * PACK : (z + 1) * P * PACK, h * HALF_N : (h + 1) * HALF_N]
+            nc.sync.dma_start(out=raw[:], in_=rows.rearrange("(p j) n -> p j n", j=PACK))
+            return raw
+
+        def load_res(c):
+            r = keep.tile([P, T], F32, name="res%d" % c)
+            nc.sync.dma_start(out=r[:], in_=res[c * P : (c + 1) * P, :])
+            return r
+
+        gb_col = load_gate(gb, "gb_col")
+        raw = {(0, z): load_wa(0, z) for z in range(PASSES)}
+        ga_col = load_gate(ga, "ga_col")
+        res_t = [load_res(0)]
+        for z in range(PASSES):
+            raw[(1, z)] = load_wa(1, z)
+        for c in range(1, TILES):
+            res_t.append(load_res(c))
+
+        nc.vector.memset(pages_b[0][:], 0.0)
+
+        def gather(src, lst, dtype, name):
+            dst = keep.tile([P, J], dtype, name=name, align_bytes=64)
+            nc.vector.tensor_copy(dst[:], src[:].indirect(lst[:]))
+            return dst
+
+        xb_scales = gather(x_scales, list_b, U8, "xb_scales")
+        nc.scalar.dma_start(
+            out=xb_scales1[0:100, :].bitcast(I32), in_=xb_scales[4:104, :].bitcast(I32)
+        )
+        xb_words = [gather(x_words[z], list_b, U32, "xb_words%d" % z) for z in range(PASSES)]
+        xa_scales = gather(x_scales, list_a, U8, "xa_scales")
+        xa_words = [gather(x_words[z], list_a, U32, "xa_words%d" % z) for z in range(PASSES)]
+
+        def late_page(name, tag):
+            page = keep.tile([P, T], F32, name=name, tag=tag, align_bytes=64)
+            nc.gpsimd.memset(page[:], 0.0)
+            return page
+
+        pages_b.append(late_page("page_b1", "x_words0"))
+        pages_a = [late_page("page_a0", "x_words1"), late_page("page_a1", "x_scales")]
+
+        def spread_gate(col, name):
+            bank = psum.tile([P, 4, P], F32, name="bank_" + name, tag="mm")
+            for m in range(4):
+                nc.tensor.transpose(bank[:, m, :], col[:, m : m + 1].to_broadcast([P, P]), ident[:])
+            row = keep.tile([P, P, 4], F32, name=name)
+            nc.scalar.copy(out=row[:], in_=bank[:].rearrange("p m n -> p n m"))
+            return row[:].rearrange("p n m -> p (n m)")
+
+        def product_b(c, tag):
+            bank = psum.tile([P, J], F32, name="bank_q%d" % c, tag="mm")
+            planes = [xb_scales[:], xb_scales1[:]]
+            for z in range(PASSES):
+                nc.tensor.matmul_mx(
+                    out=bank[:],
+                    lhsT=b_words[:, z, 2 * c * P : 2 * (c + 1) * P].bitcast(FP4X4),
+                    lhsT_scale=b_scales[:, z, c * P : (c + 1) * P],
+                    rhs=xb_words[z][:].bitcast(FP8X4),
+                    rhs_scale=planes[z],
+                    start=(z == 0),
+                    stop=(z == PASSES - 1),
+                )
+            q = keep.tile([P, J], F32, name="q%d" % c, tag=tag)
+            nc.scalar.copy(out=q[:], in_=bank[:])
+            return q
+
+        def cast_wa(h, z):
+            grouped = keep.tile([P, HALF_N, PACK], BF16, name="grouped%d%d" % (h, z), align_bytes=64)
+            nc.scalar.copy(
+                out=grouped[:].rearrange("p (c i) j -> p c j i", i=4),
+                in_=raw[(h, z)][:].rearrange("p j (c i) -> p c j i", i=4),
+            )
+            return grouped
+
+        def quantize_wa(h, z, grouped):
+            codes = keep.tile([P, HALF_N], U32, name="a_codes%d%d" % (h, z), align_bytes=64)
+            scales = keep.tile([P, HALF_N], U8, name="a_scales%d%d" % (h, z), align_bytes=64)
+            nc.vector.quantize_mx(
+                out=codes[:].bitcast(FP8X4),
+                scales=scales[:],
+                in_=grouped[:].rearrange("p n j -> p (n j)"),
+            )
+            return codes, scales
+
+        def product_a(c, sign):
+            bank = psum.tile([P, J], F32, name="bank_p%d" % c, tag="mm")
+            h, cols = c // 2, slice((c % 2) * P, (c % 2 + 1) * P)
+            for z in range(PASSES):
+                codes, scales = a_quant[(h, z)]
+                nc.tensor.matmul_mx(
+                    out=bank[:],
+                    lhsT=codes[:, cols].bitcast(FP8X4),
+                    lhsT_scale=scales[:, cols],
+                    rhs=xa_words[z][:].bitcast(FP8X4),
+                    rhs_scale=xa_scales[4 * z : P, :],
+                    start=(z == 0),
+                    stop=(z == PASSES - 1),
+                )
+            p = keep.tile([P, J], F32, name="p%d" % c)
+            nc.scalar.activation(out=p[:], in_=bank[:], func=ACT.Copy, scale=sign)
+            return p
+
+        def scatter(page, lst, values, gate):
+            nc.vector.tensor_tensor(page[:].indirect(lst[:]), values[:], gate, ALU.mult)
+
+        def turn_and_add(first, second, tag):
+            bank = psum.tile([P, BANK], F32, name="bank_" + tag, tag=tag)
+            for i, src in enumerate((first, second)):
+                for b in range(4):
+                    blk = slice(b * P, (b + 1) * P)
+                    nc.tensor.matmul(
+                        bank[:, blk], src[:, blk], ident[:],
+                        start=(i == 0 and b == 0), stop=(i == 1 and b == 3), is_transpose=True,
+                    )
+            return bank
+
+        def linear_part(c):
+            parts = []
+            for h in range(2):
+                cols = slice(h * BANK, (h + 1) * BANK)
+                bank = turn_and_add(pages_b[c % 2][:, cols], res_t[c][:, cols], "lin")
+                s = keep.tile([P, BANK], F32, name="lin%d%d" % (c, h))
+                nc.scalar.copy(out=s[:], in_=bank[:])
+                parts.append(s)
+            return parts
+
+        def finish(c, lin):
+            gains = []
+            for h in range(2):
+                cols = slice(h * BANK, (h + 1) * BANK)
+                bank = turn_and_add(pages_b[c % 2][:, cols], pages_a[c % 2][:, cols], "dif")
+                gain = ring.tile([P, BANK], F32, name="gain")
+                nc.scalar.activation(out=gain[:], in_=bank[:], func=ACT.Relu, scale=-1.0)
+                gains.append(gain)
+            for h in range(2):
+                cols = slice(h * BANK, (h + 1) * BANK)
+                bank = turn_and_add(lin[h][:], gains[h][:], "fin")
+                done = keep.tile([P, BANK], F32, name="done%d%d" % (c, h))
+                nc.scalar.copy(out=done[:], in_=bank[:])
+                nc.scalar.dma_start(out=out[c * P : (c + 1) * P, cols], in_=done[:])
+
+        a_quant = {}
+        gate_b = spread_gate(gb_col, "gate_b")
+        q0 = product_b(0, "q0")
+        scatter(pages_b[0], list_b, q0, gate_b)
+        for z in range(PASSES):
+            a_quant[(0, z)] = quantize_wa(0, z, cast_wa(0, z))
+        q1 = product_b(1, "stage01")
+        scatter(pages_b[1], list_b, q1, gate_b)
+        gate_a = spread_gate(ga_col, "gate_a")
+        p0 = product_a(0, -1.0)
+        p1 = product_a(1, -1.0)
+        lin0 = linear_part(0)
+        scatter(pages_a[0], list_a, p0, gate_a)
+        for z in range(PASSES):
+            a_quant[(1, z)] = quantize_wa(1, z, cast_wa(1, z))
+        scatter(pages_a[1], list_a, p1, gate_a)
+        q2 = product_b(2, "stage11")
+        q3 = product_b(3, "q3")
+        finish(0, lin0)
+        lin1 = linear_part(1)
+        scatter(pages_b[0], list_b, q2, gate_b)
+        p2 = product_a(2, -1.0)
+        p3 = product_a(3, 1.0)
+        finish(1, lin1)
+        scatter(pages_a[0], list_a, p2, gate_a)
+        lin2 = linear_part(2)
+        scatter(pages_b[1], list_b, q3, gate_b)
+        finish(2, lin2)
+        scatter(pages_a[1], list_a, p3, gate_a)
+
+        last = TILES - 1
+        best = keep.tile([P, T], F32, name="best")
+        total = keep.tile([P, T], F32, name="total")
+        halves = [slice(h * BANK, (h + 1) * BANK) for h in range(2)]
+        for cols in halves:
+            nc.vector.tensor_tensor(best[:, cols], pages_a[1][:, cols], pages_b[1][:, cols], ALU.max)
+        for cols in halves:
+            nc.vector.tensor_tensor(total[:, cols], best[:, cols], res_t[last][:, cols], ALU.add)
+            nc.sync.dma_start(out=out[last * P : (last + 1) * P, cols], in_=total[:, cols])

@@ -31,12 +31,11 @@ def tile_list_experts_strongest_kernel(
     nc = tc.nc
     with ExitStack() as ctx:
         keep = ctx.enter_context(tc.tile_pool(name="keep", bufs=1))
-        ring = ctx.enter_context(tc.tile_pool(name="ring", bufs=2))
-        psum = ctx.enter_context(tc.psum_pool(name="psum", bufs=2))
+        psum = ctx.enter_context(tc.psum_pool(name="psum", bufs=1))
 
         list_a = keep.tile([P, J // 16], U16, name="list_a")
         list_b = keep.tile([P, J // 16], U16, name="list_b")
-        x_words = [keep.tile([P, T], U32, name="x_words%d" % z, tag="x_words%d" % z, align_bytes=64) for z in range(PASSES)]
+        x_words = keep.tile([P, PASSES, T], U32, name="x_words", tag="x_words", align_bytes=64)
         x_scales = keep.tile([P, T], U8, name="x_scales", tag="x_scales", align_bytes=64)
         b_words = keep.tile([P, PASSES, 2 * N], U8, name="b_words", align_bytes=64)
         b_scales = keep.tile([P, PASSES, N], U8, name="b_scales", align_bytes=64)
@@ -49,80 +48,76 @@ def tile_list_experts_strongest_kernel(
         nc.vector.memset(xb_scales1[:].bitcast(I32), 0)
         make_identity(nc, ident[:])
 
-        def load_x_words(z):
-            nc.sync.dma_start(
-                out=x_words[z][:].bitcast(I32),
-                in_=xq_words[z].rearrange("p t r -> p (t r)").bitcast(I32),
-            )
-
-        nc.sync.dma_start(list_b[:], offs2)
-        load_x_words(0)
-        for q in range(4):
-            nc.sync.dma_start(
-                out=x_scales[32 * q : 32 * q + 8, :].bitcast(I32),
-                in_=xq_scales[:, 4 * q : 4 * q + 4, :].bitcast(I32),
-            )
-        load_x_words(1)
-        nc.sync.dma_start(list_a[:], offs)
-        for q in range(4):
-            nc.sync.dma_start(
-                out=b_scales[32 * q : 32 * q + 4, :, :].bitcast(I32),
-                in_=wb_scales[:, 4 * q : 4 * q + 4, :].rearrange("z r n -> r z n").bitcast(I32),
-            )
-        nc.sync.dma_start(
-            out=b_words[:].bitcast(I32), in_=wb_words.rearrange("z p n -> p z n").bitcast(I32)
-        )
-
         def load_gate(g, name):
             col = keep.tile([P, 4], F32, name=name)
             nc.sync.dma_start(out=col[:], in_=g[0].rearrange("(p m) -> p m", m=4))
             return col
 
         def load_wa(h, z):
-            raw = keep.tile([P, PACK, HALF_N], F32, name="raw%d%d" % (h, z), tag="stage%d%d" % (h, z))
+            raw = keep.tile([P, PACK, HALF_N], F32, name="raw%d%d" % (h, z), tag="stage%d%d" % (h, z), align_bytes=64)
             rows = wa[z * P * PACK : (z + 1) * P * PACK, h * HALF_N : (h + 1) * HALF_N]
             nc.sync.dma_start(out=raw[:], in_=rows.rearrange("(p j) n -> p j n", j=PACK))
             return raw
 
-        def load_res(c):
-            r = keep.tile([P, T], F32, name="res%d" % c)
-            nc.sync.dma_start(out=r[:], in_=res[c * P : (c + 1) * P, :])
-            return r
+        def load_res(c, count):
+            r = keep.tile([P, count, T], F32, name="res%d" % c)
+            rows = res[c * P : (c + count) * P, :]
+            nc.sync.dma_start(out=r[:], in_=rows.rearrange("(c p) t -> p c t", c=count))
+            return [r[:, i, :] for i in range(count)]
+
+        nc.sync.dma_start(list_b[:], offs2)
+        for q in range(4):
+            nc.sync.dma_start(
+                out=x_scales[32 * q : 32 * q + 8, :].bitcast(I32),
+                in_=xq_scales[:, 4 * q : 4 * q + 4, :].bitcast(I32),
+            )
+        nc.sync.dma_start(list_a[:], offs)
+        nc.sync.dma_start(
+            out=x_words[:].bitcast(I32),
+            in_=xq_words.rearrange("z p t r -> p z (t r)").bitcast(I32),
+        )
+        raw = {(0, z): load_wa(0, z) for z in range(PASSES)}
+        nc.sync.dma_start(
+            out=b_words[:].bitcast(I32), in_=wb_words.rearrange("z p n -> p z n").bitcast(I32)
+        )
+        for q in range(4):
+            nc.sync.dma_start(
+                out=b_scales[32 * q : 32 * q + 4, :, :].bitcast(I32),
+                in_=wb_scales[:, 4 * q : 4 * q + 4, :].rearrange("z r n -> r z n").bitcast(I32),
+            )
 
         gb_col = load_gate(gb, "gb_col")
-        raw = {(0, z): load_wa(0, z) for z in range(PASSES)}
         ga_col = load_gate(ga, "ga_col")
-        res_t = [load_res(0)]
+        res_t = load_res(0, 1)
         for z in range(PASSES):
             raw[(1, z)] = load_wa(1, z)
-        for c in range(1, TILES):
-            res_t.append(load_res(c))
+        res_t = res_t + load_res(1, 1) + load_res(2, 2)
 
         nc.vector.memset(pages_b[0][:], 0.0)
+        page_a1 = keep.tile([P, T], F32, name="page_a1")
+        nc.vector.memset(page_a1[:], 0.0)
 
         def gather(src, lst, dtype, name):
             dst = keep.tile([P, J], dtype, name=name, align_bytes=64)
-            nc.vector.tensor_copy(dst[:], src[:].indirect(lst[:]))
+            nc.vector.tensor_copy(dst[:], src.indirect(lst[:]))
             return dst
 
-        xb_scales = gather(x_scales, list_b, U8, "xb_scales")
+        xb_scales = gather(x_scales[:], list_b, U8, "xb_scales")
         nc.scalar.dma_start(
             out=xb_scales1[0:100, :].bitcast(I32), in_=xb_scales[4:104, :].bitcast(I32)
         )
-        xb_words = [gather(x_words[z], list_b, U32, "xb_words%d" % z) for z in range(PASSES)]
-        xa_scales = gather(x_scales, list_a, U8, "xa_scales")
-        xa_words = [gather(x_words[z], list_a, U32, "xa_words%d" % z) for z in range(PASSES)]
+        xb_words = [gather(x_words[:, z, :], list_b, U32, "xb_words%d" % z) for z in range(PASSES)]
+        xa_scales = gather(x_scales[:], list_a, U8, "xa_scales")
+        xa_words = [gather(x_words[:, z, :], list_a, U32, "xa_words%d" % z) for z in range(PASSES)]
 
         def late_page(name, tag):
             page = keep.tile([P, T], F32, name=name, tag=tag, align_bytes=64)
             nc.gpsimd.memset(page[:], 0.0)
             return page
 
-        pages_b.append(late_page("page_b1", "x_words0"))
-        pages_a = [late_page("page_a0", "x_words1"), late_page("page_a1", "x_scales")]
 
-        def spread_gate(col, name):
-            bank = psum.tile([P, 4, P], F32, name="bank_" + name, tag="mm")
+        def spread_gate(col, name, tag):
+            bank = psum.tile([P, 4, P], F32, name="bank_" + name, tag=tag)
             for m in range(4):
                 nc.tensor.transpose(bank[:, m, :], col[:, m : m + 1].to_broadcast([P, P]), ident[:])
             row = keep.tile([P, P, 4], F32, name=name)
@@ -130,7 +125,7 @@ def tile_list_experts_strongest_kernel(
             return row[:].rearrange("p n m -> p (n m)")
 
         def product_b(c, tag):
-            bank = psum.tile([P, J], F32, name="bank_q%d" % c, tag="mm")
+            bank = psum.tile([P, J], F32, name="bank_q%d" % c, tag="bank%d" % (c % 2))
             planes = [xb_scales[:], xb_scales1[:]]
             for z in range(PASSES):
                 nc.tensor.matmul_mx(
@@ -142,12 +137,12 @@ def tile_list_experts_strongest_kernel(
                     start=(z == 0),
                     stop=(z == PASSES - 1),
                 )
-            q = keep.tile([P, J], F32, name="q%d" % c, tag=tag)
+            q = keep.tile([P, J], F32, name="q%d" % c, tag=tag, align_bytes=64)
             nc.scalar.copy(out=q[:], in_=bank[:])
             return q
 
         def cast_wa(h, z):
-            grouped = keep.tile([P, HALF_N, PACK], BF16, name="grouped%d%d" % (h, z), align_bytes=64)
+            grouped = keep.tile([P, HALF_N, PACK], BF16, name="grouped%d%d" % (h, z), tag="grouped%d%d" % (h, z), align_bytes=64)
             nc.scalar.copy(
                 out=grouped[:].rearrange("p (c i) j -> p c j i", i=4),
                 in_=raw[(h, z)][:].rearrange("p j (c i) -> p c j i", i=4),
@@ -164,8 +159,14 @@ def tile_list_experts_strongest_kernel(
             )
             return codes, scales
 
-        def product_a(c, sign):
-            bank = psum.tile([P, J], F32, name="bank_p%d" % c, tag="mm")
+        turns = []
+
+        def next_bank():
+            turns.append(None)
+            return ("bank3", "bank4", "bank5")[len(turns) % 3]
+
+        def product_a(c, sign, tag):
+            bank = psum.tile([P, J], F32, name="bank_p%d" % c, tag=("bank%d" % c if c < 2 else next_bank()))
             h, cols = c // 2, slice((c % 2) * P, (c % 2 + 1) * P)
             for z in range(PASSES):
                 codes, scales = a_quant[(h, z)]
@@ -178,7 +179,7 @@ def tile_list_experts_strongest_kernel(
                     start=(z == 0),
                     stop=(z == PASSES - 1),
                 )
-            p = keep.tile([P, J], F32, name="p%d" % c)
+            p = keep.tile([P, J], F32, name="p%d" % c, tag=tag, align_bytes=64)
             nc.scalar.activation(out=p[:], in_=bank[:], func=ACT.Copy, scale=sign)
             return p
 
@@ -186,7 +187,7 @@ def tile_list_experts_strongest_kernel(
             nc.vector.tensor_tensor(page[:].indirect(lst[:]), values[:], gate, ALU.mult)
 
         def turn_and_add(first, second, tag):
-            bank = psum.tile([P, BANK], F32, name="bank_" + tag, tag=tag)
+            bank = psum.tile([P, BANK], F32, name="bank_" + tag, tag=next_bank())
             for i, src in enumerate((first, second)):
                 for b in range(4):
                     blk = slice(b * P, (b + 1) * P)
@@ -206,14 +207,20 @@ def tile_list_experts_strongest_kernel(
                 parts.append(s)
             return parts
 
-        def finish(c, lin):
+        def gain_part(c):
             gains = []
             for h in range(2):
                 cols = slice(h * BANK, (h + 1) * BANK)
-                bank = turn_and_add(pages_b[c % 2][:, cols], pages_a[c % 2][:, cols], "dif")
-                gain = ring.tile([P, BANK], F32, name="gain")
+                pair = [pages_a[c % 2][:, cols], pages_b[c % 2][:, cols]]
+                if c == TILES - 2:
+                    pair = [pair[1], pair[0]]
+                bank = turn_and_add(pair[0], pair[1], "dif")
+                gain = keep.tile([P, BANK], F32, name="gain%d%d" % (c, h))
                 nc.scalar.activation(out=gain[:], in_=bank[:], func=ACT.Relu, scale=-1.0)
                 gains.append(gain)
+            return gains
+
+        def finish(c, lin, gains):
             for h in range(2):
                 cols = slice(h * BANK, (h + 1) * BANK)
                 bank = turn_and_add(lin[h][:], gains[h][:], "fin")
@@ -222,33 +229,35 @@ def tile_list_experts_strongest_kernel(
                 nc.scalar.dma_start(out=out[c * P : (c + 1) * P, cols], in_=done[:])
 
         a_quant = {}
-        gate_b = spread_gate(gb_col, "gate_b")
-        q0 = product_b(0, "q0")
-        scatter(pages_b[0], list_b, q0, gate_b)
         for z in range(PASSES):
             a_quant[(0, z)] = quantize_wa(0, z, cast_wa(0, z))
-        q1 = product_b(1, "stage01")
-        scatter(pages_b[1], list_b, q1, gate_b)
-        gate_a = spread_gate(ga_col, "gate_a")
-        p0 = product_a(0, -1.0)
-        p1 = product_a(1, -1.0)
-        lin0 = linear_part(0)
+        pages_a = [late_page("page_a0", "grouped01"), page_a1]
+        gate_b = spread_gate(gb_col, "gate_b", "bank2")
+        q0 = product_b(0, "q0")
+        scatter(pages_b[0], list_b, q0, gate_b)
+        pages_b.append(late_page("page_b1", "q0"))
+        q1 = product_b(1, "q1")
+        gate_a = spread_gate(ga_col, "gate_a", "bank2")
+        p0 = product_a(0, -1.0, "p0")
         scatter(pages_a[0], list_a, p0, gate_a)
+        p1 = product_a(1, -1.0, "p1")
+        scatter(pages_b[1], list_b, q1, gate_b)
+        scatter(pages_a[1], list_a, p1, gate_a)
         for z in range(PASSES):
             a_quant[(1, z)] = quantize_wa(1, z, cast_wa(1, z))
-        scatter(pages_a[1], list_a, p1, gate_a)
         q2 = product_b(2, "stage11")
         q3 = product_b(3, "q3")
-        finish(0, lin0)
-        lin1 = linear_part(1)
+        lin0 = linear_part(0)
+        finish(0, lin0, gain_part(0))
         scatter(pages_b[0], list_b, q2, gate_b)
-        p2 = product_a(2, -1.0)
-        p3 = product_a(3, 1.0)
-        finish(1, lin1)
+        lin1 = linear_part(1)
+        p2 = product_a(2, -1.0, "p2")
+        p3 = product_a(3, 1.0, "p3")
         scatter(pages_a[0], list_a, p2, gate_a)
-        lin2 = linear_part(2)
+        finish(1, lin1, gain_part(1))
         scatter(pages_b[1], list_b, q3, gate_b)
-        finish(2, lin2)
+        lin2 = linear_part(2)
+        finish(2, lin2, gain_part(2))
         scatter(pages_a[1], list_a, p3, gate_a)
 
         last = TILES - 1
@@ -257,6 +266,6 @@ def tile_list_experts_strongest_kernel(
         halves = [slice(h * BANK, (h + 1) * BANK) for h in range(2)]
         for cols in halves:
             nc.vector.tensor_tensor(best[:, cols], pages_a[1][:, cols], pages_b[1][:, cols], ALU.max)
-        for cols in halves:
+        for cols in (halves[0], slice(BANK, BANK + 256), slice(BANK + 256, T)):
             nc.vector.tensor_tensor(total[:, cols], best[:, cols], res_t[last][:, cols], ALU.add)
             nc.sync.dma_start(out=out[last * P : (last + 1) * P, cols], in_=total[:, cols])

@@ -72,6 +72,7 @@ def tile_list_experts_strongest_kernel(
                 in_=xq_scales[:, 4 * q : 4 * q + 4, :].bitcast(I32),
             )
         nc.sync.dma_start(list_a[:], offs)
+        gb_col = load_gate(gb, "gb_col")
         nc.sync.dma_start(
             out=x_words[:].bitcast(I32),
             in_=xq_words.rearrange("z p t r -> p z (t r)").bitcast(I32),
@@ -86,16 +87,13 @@ def tile_list_experts_strongest_kernel(
                 in_=wb_scales[:, 4 * q : 4 * q + 4, :].rearrange("z r n -> r z n").bitcast(I32),
             )
 
-        gb_col = load_gate(gb, "gb_col")
         ga_col = load_gate(ga, "ga_col")
         res_t = load_res(0, 1)
         for z in range(PASSES):
             raw[(1, z)] = load_wa(1, z)
         res_t = res_t + load_res(1, 1) + load_res(2, 2)
 
-        nc.vector.memset(pages_b[0][:], 0.0)
-        page_a1 = keep.tile([P, T], F32, name="page_a1")
-        nc.vector.memset(page_a1[:], 0.0)
+        nc.gpsimd.memset(pages_b[0][:], 0.0)
 
         def gather(src, lst, dtype, name):
             dst = keep.tile([P, J], dtype, name=name, align_bytes=64)
@@ -231,7 +229,7 @@ def tile_list_experts_strongest_kernel(
         a_quant = {}
         for z in range(PASSES):
             a_quant[(0, z)] = quantize_wa(0, z, cast_wa(0, z))
-        pages_a = [late_page("page_a0", "grouped01"), page_a1]
+        pages_a = [late_page("page_a0", "grouped01")]
         gate_b = spread_gate(gb_col, "gate_b", "bank2")
         q0 = product_b(0, "q0")
         scatter(pages_b[0], list_b, q0, gate_b)
@@ -240,6 +238,7 @@ def tile_list_experts_strongest_kernel(
         gate_a = spread_gate(ga_col, "gate_a", "bank2")
         p0 = product_a(0, -1.0, "p0")
         scatter(pages_a[0], list_a, p0, gate_a)
+        pages_a.append(late_page("page_a1", "p0"))
         p1 = product_a(1, -1.0, "p1")
         scatter(pages_b[1], list_b, q1, gate_b)
         scatter(pages_a[1], list_a, p1, gate_a)

from contextlib import ExitStack

import concourse.mybir as mybir
from concourse.masks import make_identity

K, T, J, N = 1024, 1024, 512, 512
FLOPS = 2 * 2 * K * J * N

F32 = mybir.dt.float32
BF16 = mybir.dt.bfloat16
I32 = mybir.dt.int32
U32 = mybir.dt.uint32
U16 = mybir.dt.uint16
U8 = mybir.dt.uint8
FP8X4 = mybir.dt.float8_e4m3fn_x4
FP4X4 = mybir.dt.float4_e2m1fn_x4
ALU = mybir.AluOpType
ACT = mybir.ActivationFunctionType

P = 128
PACK = 4
PASSES = K // (P * PACK)
TILES = N // P
BANK = 512
HALF_N = N // 2


def tile_list_experts_strongest_kernel(
    tc, xq_words, xq_scales, wa, wb_words, wb_scales, ga, gb, res, offs, offs2, out
):
    nc = tc.nc
    with ExitStack() as ctx:
        keep = ctx.enter_context(tc.tile_pool(name="keep", bufs=1))
        psum = ctx.enter_context(tc.psum_pool(name="psum", bufs=1))

        list_a = keep.tile([P, J // 16], U16, name="list_a")
        list_b = keep.tile([P, J // 16], U16, name="list_b")
        x_words = keep.tile([P, PASSES, T], U32, name="x_words", tag="x_words", align_bytes=64)
        x_scales = keep.tile([P, T], U8, name="x_scales", tag="x_scales", align_bytes=64)
        b_words = keep.tile([P, PASSES, 2 * N], U8, name="b_words", align_bytes=64)
        b_scales = keep.tile([P, PASSES, N], U8, name="b_scales", align_bytes=64)
        xb_scales1 = keep.tile([P, J], U8, name="xb_scales1", align_bytes=64)
        pages_b = [keep.tile([P, T], F32, name="page_b0")]
        ident = keep.tile([P, P], F32, name="ident")

        nc.vector.memset(x_scales[:].bitcast(I32), 0)
        nc.vector.memset(b_scales[:].rearrange("p z n -> p (z n)").bitcast(I32), 0)
        nc.vector.memset(xb_scales1[:].bitcast(I32), 0)
        make_identity(nc, ident[:])

        def load_gate(g, name):
            col = keep.tile([P, 4], F32, name=name)
            nc.sync.dma_start(out=col[:], in_=g[0].rearrange("(p m) -> p m", m=4))
            return col

        def load_wa(h, z):
            raw = keep.tile([P, PACK, HALF_N], F32, name="raw%d%d" % (h, z), tag="stage%d%d" % (h, z), align_bytes=64)
            rows = wa[z * P * PACK : (z + 1) * P * PACK, h * HALF_N : (h + 1) * HALF_N]
            nc.sync.dma_start(out=raw[:], in_=rows.rearrange("(p j) n -> p j n", j=PACK))
            return raw

        def load_res(c, count):
            r = keep.tile([P, count, T], F32, name="res%d" % c)
            rows = res[c * P : (c + count) * P, :]
            nc.sync.dma_start(out=r[:], in_=rows.rearrange("(c p) t -> p c t", c=count))
            return [r[:, i, :] for i in range(count)]

        nc.sync.dma_start(list_b[:], offs2)
        for q in range(4):
            nc.sync.dma_start(
                out=x_scales[32 * q : 32 * q + 8, :].bitcast(I32),
                in_=xq_scales[:, 4 * q : 4 * q + 4, :].bitcast(I32),
            )
        nc.sync.dma_start(list_a[:], offs)
        gb_col = load_gate(gb, "gb_col")
        nc.sync.dma_start(
            out=x_words[:].bitcast(I32),
            in_=xq_words.rearrange("z p t r -> p z (t r)").bitcast(I32),
        )
        raw = {(0, z): load_wa(0, z) for z in range(PASSES)}
        nc.sync.dma_start(
            out=b_words[:].bitcast(I32), in_=wb_words.rearrange("z p n -> p z n").bitcast(I32)
        )
        for q in range(4):
            nc.sync.dma_start(
                out=b_scales[32 * q : 32 * q + 4, :, :].bitcast(I32),
                in_=wb_scales[:, 4 * q : 4 * q + 4, :].rearrange("z r n -> r z n").bitcast(I32),
            )

        ga_col = load_gate(ga, "ga_col")
        res_t = load_res(0, 1)
        for z in range(PASSES):
            raw[(1, z)] = load_wa(1, z)
        res_t = res_t + load_res(1, 1) + load_res(2, 2)

        nc.gpsimd.memset(pages_b[0][:], 0.0)

        def gather(src, lst, dtype, name):
            dst = keep.tile([P, J], dtype, name=name, align_bytes=64)
            nc.vector.tensor_copy(dst[:], src.indirect(lst[:]))
            return dst

        xb_scales = gather(x_scales[:], list_b, U8, "xb_scales")
        nc.scalar.dma_start(
            out=xb_scales1[0:100, :].bitcast(I32), in_=xb_scales[4:104, :].bitcast(I32)
        )
        xb_words = [gather(x_words[:, z, :], list_b, U32, "xb_words%d" % z) for z in range(PASSES)]
        xa_scales = gather(x_scales[:], list_a, U8, "xa_scales")
        xa_words = [gather(x_words[:, z, :], list_a, U32, "xa_words%d" % z) for z in range(PASSES)]

        def late_page(name, tag):
            page = keep.tile([P, T], F32, name=name, tag=tag, align_bytes=64)
            nc.gpsimd.memset(page[:], 0.0)
            return page


        def spread_gate(col, name, tag):
            bank = psum.tile([P, 4, P], F32, name="bank_" + name, tag=tag)
            for m in range(4):
                nc.tensor.transpose(bank[:, m, :], col[:, m : m + 1].to_broadcast([P, P]), ident[:])
            row = keep.tile([P, P, 4], F32, name=name)
            nc.scalar.copy(out=row[:], in_=bank[:].rearrange("p m n -> p n m"))
            return row[:].rearrange("p n m -> p (n m)")

        def product_b(c, tag):
            bank = psum.tile([P, J], F32, name="bank_q%d" % c, tag="bank%d" % (c % 2))
            planes = [xb_scales[:], xb_scales1[:]]
            for z in range(PASSES):
                nc.tensor.matmul_mx(
                    out=bank[:],
                    lhsT=b_words[:, z, 2 * c * P : 2 * (c + 1) * P].bitcast(FP4X4),
                    lhsT_scale=b_scales[:, z, c * P : (c + 1) * P],
                    rhs=xb_words[z][:].bitcast(FP8X4),
                    rhs_scale=planes[z],
                    start=(z == 0),
                    stop=(z == PASSES - 1),
                )
            q = keep.tile([P, J], F32, name="q%d" % c, tag=tag, align_bytes=64)
            nc.scalar.copy(out=q[:], in_=bank[:])
            return q

        def cast_wa(h, z):
            grouped = keep.tile([P, HALF_N, PACK], BF16, name="grouped%d%d" % (h, z), tag="grouped%d%d" % (h, z), align_bytes=64)
            nc.scalar.copy(
                out=grouped[:].rearrange("p (c i) j -> p c j i", i=4),
                in_=raw[(h, z)][:].rearrange("p j (c i) -> p c j i", i=4),
            )
            return grouped

        def quantize_wa(h, z, grouped):
            codes = keep.tile([P, HALF_N], U32, name="a_codes%d%d" % (h, z), align_bytes=64)
            scales = keep.tile([P, HALF_N], U8, name="a_scales%d%d" % (h, z), align_bytes=64)
            nc.vector.quantize_mx(
                out=codes[:].bitcast(FP8X4),
                scales=scales[:],
                in_=grouped[:].rearrange("p n j -> p (n j)"),
            )
            return codes, scales

        turns = []

        def next_bank():
            turns.append(None)
            return ("bank3", "bank4", "bank5")[len(turns) % 3]

        def product_a(c, sign, tag):
            bank = psum.tile([P, J], F32, name="bank_p%d" % c, tag=("bank%d" % c if c < 2 else next_bank()))
            h, cols = c // 2, slice((c % 2) * P, (c % 2 + 1) * P)
            for z in range(PASSES):
                codes, scales = a_quant[(h, z)]
                nc.tensor.matmul_mx(
                    out=bank[:],
                    lhsT=codes[:, cols].bitcast(FP8X4),
                    lhsT_scale=scales[:, cols],
                    rhs=xa_words[z][:].bitcast(FP8X4),
                    rhs_scale=xa_scales[4 * z : P, :],
                    start=(z == 0),
                    stop=(z == PASSES - 1),
                )
            p = keep.tile([P, J], F32, name="p%d" % c, tag=tag, align_bytes=64)
            nc.scalar.activation(out=p[:], in_=bank[:], func=ACT.Copy, scale=sign)
            return p

        def scatter(page, lst, values, gate):
            nc.vector.tensor_tensor(page[:].indirect(lst[:]), values[:], gate, ALU.mult)

        def turn_and_add(first, second, tag):
            bank = psum.tile([P, BANK], F32, name="bank_" + tag, tag=next_bank())
            for i, src in enumerate((first, second)):
                for b in range(4):
                    blk = slice(b * P, (b + 1) * P)
                    nc.tensor.matmul(
                        bank[:, blk], src[:, blk], ident[:],
                        start=(i == 0 and b == 0), stop=(i == 1 and b == 3), is_transpose=True,
                    )
            return bank

        def linear_part(c):
            parts = []
            for h in range(2):
                cols = slice(h * BANK, (h + 1) * BANK)
                bank = turn_and_add(pages_b[c % 2][:, cols], res_t[c][:, cols], "lin")
                s = keep.tile([P, BANK], F32, name="lin%d%d" % (c, h))
                nc.scalar.copy(out=s[:], in_=bank[:])
                parts.append(s)
            return parts

        def gain_part(c):
            gains = []
            for h in range(2):
                cols = slice(h * BANK, (h + 1) * BANK)
                pair = [pages_a[c % 2][:, cols], pages_b[c % 2][:, cols]]
                if c == TILES - 2:
                    pair = [pair[1], pair[0]]
                bank = turn_and_add(pair[0], pair[1], "dif")
                gain = keep.tile([P, BANK], F32, name="gain%d%d" % (c, h))
                nc.scalar.activation(out=gain[:], in_=bank[:], func=ACT.Relu, scale=-1.0)
                gains.append(gain)
            return gains

        def finish(c, lin, gains):
            for h in range(2):
                cols = slice(h * BANK, (h + 1) * BANK)
                bank = turn_and_add(lin[h][:], gains[h][:], "fin")
                done = keep.tile([P, BANK], F32, name="done%d%d" % (c, h))
                nc.scalar.copy(out=done[:], in_=bank[:])
                nc.scalar.dma_start(out=out[c * P : (c + 1) * P, cols], in_=done[:])

        a_quant = {}
        for z in range(PASSES):
            a_quant[(0, z)] = quantize_wa(0, z, cast_wa(0, z))
        pages_a = [late_page("page_a0", "grouped01")]
        gate_b = spread_gate(gb_col, "gate_b", "bank2")
        q0 = product_b(0, "q0")
        scatter(pages_b[0], list_b, q0, gate_b)
        pages_b.append(late_page("page_b1", "q0"))
        q1 = product_b(1, "q1")
        gate_a = spread_gate(ga_col, "gate_a", "bank2")
        p0 = product_a(0, -1.0, "p0")
        scatter(pages_a[0], list_a, p0, gate_a)
        pages_a.append(late_page("page_a1", "p0"))
        p1 = product_a(1, -1.0, "p1")
        scatter(pages_b[1], list_b, q1, gate_b)
        scatter(pages_a[1], list_a, p1, gate_a)
        for z in range(PASSES):
            a_quant[(1, z)] = quantize_wa(1, z, cast_wa(1, z))
        q2 = product_b(2, "stage11")
        q3 = product_b(3, "q3")
        lin0 = linear_part(0)
        finish(0, lin0, gain_part(0))
        scatter(pages_b[0], list_b, q2, gate_b)
        lin1 = linear_part(1)
        p2 = product_a(2, -1.0, "p2")
        p3 = product_a(3, 1.0, "p3")
        scatter(pages_a[0], list_a, p2, gate_a)
        finish(1, lin1, gain_part(1))
        scatter(pages_b[1], list_b, q3, gate_b)
        lin2 = linear_part(2)
        finish(2, lin2, gain_part(2))
        scatter(pages_a[1], list_a, p3, gate_a)

        last = TILES - 1
        best = keep.tile([P, T], F32, name="best")
        total = keep.tile([P, T], F32, name="total")
        halves = [slice(h * BANK, (h + 1) * BANK) for h in range(2)]
        for cols in halves:
            nc.vector.tensor_tensor(best[:, cols], pages_a[1][:, cols], pages_b[1][:, cols], ALU.max)
        for cols in (halves[0], slice(BANK, BANK + 256), slice(BANK + 256, T)):
            nc.vector.tensor_tensor(total[:, cols], best[:, cols], res_t[last][:, cols], ALU.add)
            nc.sync.dma_start(out=out[last * P : (last + 1) * P, cols], in_=total[:, cols])
